import numpy as np
import ml_dtypes


def mxq(x, axis, fmt="e4m3"):
    dtype, down = {"e4m3": (ml_dtypes.float8_e4m3fn, 7), "e5m2": (ml_dtypes.float8_e5m2, 14)}[fmt]
    v = np.moveaxis(np.asarray(x, np.float32).astype(ml_dtypes.bfloat16).astype(np.float64), axis, -1)
    blocks = v.reshape(v.shape[:-1] + (-1, 32))
    amax = np.abs(blocks).max(-1, keepdims=True)
    byte = np.maximum(np.where(amax > 0, np.frexp(amax)[1] - 1 + 127, 0) - down, 1)
    scale = np.exp2(byte - 127.0)
    codes = (blocks / scale).astype(np.float32).astype(dtype).astype(np.float64)
    return np.moveaxis((codes * scale).reshape(v.shape), -1, axis)


WIDE = False


def mx_kscale(k):
    if not WIDE:
        return np.ones(k)
    levels = np.array([18, -18])
    if k % 512:
        return np.exp2(np.random.permutation(np.resize(levels, k // 32))).repeat(32)
    a = np.empty((k // 512, 16))
    for p in range(k // 512):
        a[p, :8] = np.random.permutation(np.resize(levels, 8))
        for g in range(8):
            far = levels[np.abs(levels - a[p, g]) >= 10]
            a[p, g + 8] = far[np.random.randint(len(far))]
    return np.exp2(a.ravel()).repeat(32)


def f64(x):
    return np.asarray(x).astype(np.float64)


def striped(idx):
    return np.tile(np.asarray(idx).reshape(-1, 16).T, (8, 1)).astype(np.uint16)


def unstriped(offs):
    return offs[:16].T.reshape(-1).astype(np.int64)


B, N, T, D, R = 1, 512, 2048, 1024, 512


def setup_inputs():
    n = np.random.standard_normal
    idx = np.random.permutation(T)[:B * N]
    s = mx_kscale(D)[:, None]
    z = mx_kscale(R)[:, None]
    x = n((B, D, R))
    teach = np.exp(n((B, R, N)))
    teach = teach / teach.sum(-1, keepdims=True)
    return {
        "xT": (x * s).astype(np.float32),
        "wT": (n((D, T)) * (0.50 / np.sqrt(D)) / s).astype(np.float32),
        "y": teach.astype(np.float32),
        "lse": (np.log(N) + 0.12 + 0.1 * n((B, R, 1))).astype(np.float32),
        "wt": (np.random.uniform(0.5, 1.5, (B, R, 1)) * N / np.sqrt(R) * z).astype(np.float32),
        "xm": (x.transpose(0, 2, 1) / z).astype(np.float32),
        "offs": striped(idx),
    }


def reference(xT, wT, y, lse, wt, xm, offs):
    idx = unstriped(offs)
    pick = lambda x: x[:, idx].reshape(x.shape[0], B, N).transpose(1, 0, 2)
    a = mxq(f64(xT), 1, "e4m3").transpose(0, 2, 1) @ mxq(pick(f64(wT)), 1, "e4m3")
    g = f64(wt) * (np.exp(a - f64(lse)) - f64(y))
    dw = mxq(f64(xm), 1, "e4m3").transpose(0, 2, 1) @ mxq(g, 1, "e5m2")
    gw = np.zeros((D, T))
    gw[:, idx] = dw.transpose(1, 0, 2).reshape(D, B * N)
    return gw

@@ -1,0 +1,199 @@
+from contextlib import ExitStack
+
+import concourse.mybir as mybir
+
+N, T, D, R = 512, 2048, 1024, 512
+FLOPS = 2 * 2 * N * D * R
+
+F32 = mybir.dt.float32
+BF16 = mybir.dt.bfloat16
+U32 = mybir.dt.uint32
+U16 = mybir.dt.uint16
+U8 = mybir.dt.uint8
+E4M3 = mybir.dt.float8_e4m3fn_x4
+E5M2 = mybir.dt.float8_e5m2_x4
+ACT = mybir.ActivationFunctionType
+ALU = mybir.AluOpType
+
+P = 128
+PACK = 4
+K_PASS = P * PACK
+PASSES = D // K_PASS
+HALF = R // 2
+D_TILES = D // P
+WINDOWS = 4
+XM_CHUNKS = ((0, 256), (256, 512), (512, 1024))
+
+
+def tile_attend_glse_w_kernel(tc, xT, wT, y, lse, wt, xm, offs, out):
+    nc = tc.nc
+    with ExitStack() as ctx:
+        keep = ctx.enter_context(tc.tile_pool(name="keep", bufs=1))
+        ring = ctx.enter_context(tc.tile_pool(name="ring", bufs=3))
+        psum_a = ctx.enter_context(tc.psum_pool(name="psum_a", bufs=1))
+        psum_o = ctx.enter_context(tc.psum_pool(name="psum_o", bufs=4))
+
+        offsets = keep.tile([P, N // 16], U16, name="offsets")
+        w_raw = [keep.tile([P, T], F32, name="w_raw%d" % u) for u in range(PASSES * PACK)]
+        x_raw = [keep.tile([P, PACK, HALF], F32, name="x_raw%d" % u) for u in range(PASSES * 2)]
+        y_raw = [keep.tile([P, 2, N], F32, name="y_raw%d" % u) for u in range(2)]
+        xm_raw = [keep.tile([P, PACK, b - a], F32, name="xm_raw%d" % a) for a, b in XM_CHUNKS]
+        lse_sb = keep.tile([P, PACK], F32, name="lse_sb")
+        neg_lse = keep.tile([P, PACK], F32, name="neg_lse")
+        wt_sb = keep.tile([P, PACK], F32, name="wt_sb")
+        windows = [keep.tile([P, T], F32, name="window%d" % u) for u in range(WINDOWS)]
+
+        w_planes = wT.rearrange("(g p t) c -> g t p c", p=P, t=PACK)
+        x_rows = xT[0].rearrange("(g p t) r -> g p t r", p=P, t=PACK)
+        y_rows = y[0].rearrange("(p j) i -> p j i", j=PACK)
+        xm_rows = xm[0].rearrange("(p j) d -> p j d", j=PACK)
+
+        def load_w(u):
+            nc.sync.dma_start(out=w_raw[u][:], in_=w_planes[u // PACK, u % PACK])
+
+        def load_x(u):
+            g, h = divmod(u, 2)
+            nc.sync.dma_start(out=x_raw[u][:], in_=x_rows[g][:, :, h * HALF : (h + 1) * HALF])
+
+        load_w(0)
+        nc.sync.dma_start(offsets[:], offs)
+        nc.sync.dma_start(out=lse_sb[:], in_=lse[0].rearrange("(p j) o -> p (j o)", j=PACK))
+        nc.sync.dma_start(out=wt_sb[:], in_=wt[0].rearrange("(p j) o -> p (j o)", j=PACK))
+        load_x(0)
+        for u in range(1, PASSES * PACK):
+            load_w(u)
+        for u in range(1, PASSES * 2):
+            load_x(u)
+        for u in range(2):
+            nc.sync.dma_start(out=y_raw[u][:], in_=y_rows[:, 2 * u : 2 * u + 2, :])
+        for c, (a, b) in enumerate(XM_CHUNKS):
+            nc.sync.dma_start(out=xm_raw[c][:], in_=xm_rows[:, :, a:b])
+
+        for window in windows:
+            nc.vector.memset(window[:], 0.0)
+        nc.scalar.activation(neg_lse[:], lse_sb[:], ACT.Copy, scale=-1.0)
+
+        w_bf = [keep.tile([P, N, PACK], BF16, name="w_bf%d" % g, align_bytes=64) for g in range(PASSES)]
+        w_codes = [keep.tile([P, N], U32, name="w_codes%d" % g, align_bytes=64) for g in range(PASSES)]
+        w_scales = [keep.tile([P, N], U8, name="w_scales%d" % g, align_bytes=64) for g in range(PASSES)]
+        x_bf = [keep.tile([P, PACK, P, PACK], BF16, name="x_bf%d" % g, align_bytes=64) for g in range(PASSES)]
+        x_codes = [keep.tile([P, R], U32, name="x_codes%d" % g, align_bytes=64) for g in range(PASSES)]
+        x_scales = [keep.tile([P, R], U8, name="x_scales%d" % g, align_bytes=64) for g in range(PASSES)]
+
+        def gather_w(u):
+            nc.vector.tensor_copy(w_bf[u // PACK][:, :, u % PACK], w_raw[u][:].indirect(offsets[:]))
+
+        def quantize_w(g):
+            nc.vector.quantize_mx(
+                out=w_codes[g][:].bitcast(E4M3), scales=w_scales[g][:], in_=w_bf[g][:].rearrange("p n t -> p (n t)")
+            )
+
+        def weave_x(u, copy):
+            g, h = divmod(u, 2)
+            s_cols = slice(h * P // 2, (h + 1) * P // 2)
+            copy(
+                x_bf[g][:, :, s_cols, :].rearrange("p j s t -> p s t j"),
+                x_raw[u][:].rearrange("p t (s j) -> p s t j", j=PACK),
+            )
+
+        def quantize_x(g, j0, j1):
+            cols = slice(j0 * P, j1 * P)
+            nc.vector.quantize_mx(
+                out=x_codes[g][:, cols].bitcast(E4M3),
+                scales=x_scales[g][:, cols],
+                in_=x_bf[g][:, j0:j1].rearrange("p j s t -> p (j s t)"),
+            )
+
+        scores = [psum_a.tile([P, N], F32, name="score%d" % j) for j in range(PACK)]
+
+        def score_pass(g, j):
+            cols = slice(j * P, (j + 1) * P)
+            nc.tensor.matmul_mx(
+                out=scores[j][:],
+                lhsT=x_codes[g][:, cols].bitcast(E4M3),
+                lhsT_scale=x_scales[g][:, cols],
+                rhs=w_codes[g][:].bitcast(E4M3),
+                rhs_scale=w_scales[g][:],
+                start=(g == 0),
+                stop=(g == PASSES - 1),
+            )
+
+        weave_x(0, nc.scalar.copy)
+        for u in range(PACK):
+            gather_w(u)
+        quantize_w(0)
+        for u in range(PACK, 2 * PACK):
+            gather_w(u)
+        weave_x(1, nc.scalar.copy)
+        weave_x(2, nc.scalar.copy)
+        quantize_w(1)
+        quantize_x(0, 0, PACK)
+        for j in range(PACK):
+            score_pass(0, j)
+        weave_x(3, nc.vector.tensor_copy)
+        for j in range(PACK):
+            quantize_x(1, j, j + 1)
+            score_pass(1, j)
+
+        yw = keep.tile([P, PACK, N], F32, name="yw")
+        prob = keep.tile([P, PACK, N], F32, name="prob")
+        g_planes = keep.tile([P, PACK, N], BF16, name="g_planes")
+        g_bf = keep.tile([P, N, PACK], BF16, name="g_bf", align_bytes=64)
+        g_codes = keep.tile([P, N], U32, name="g_codes", align_bytes=64)
+        g_scales = keep.tile([P, N], U8, name="g_scales", align_bytes=64)
+        for j in range(PACK):
+            nc.scalar.activation(prob[:, j, :], scores[j][:], ACT.Exp, bias=neg_lse[:, j : j + 1])
+            nc.vector.tensor_scalar(yw[:, j, :], y_raw[j // 2][:, j % 2, :], wt_sb[:, j : j + 1], None, ALU.mult)
+        for j in range(PACK):
+            nc.vector.scalar_tensor_tensor(
+                g_planes[:, j, :], prob[:, j, :], wt_sb[:, j : j + 1], yw[:, j, :], ALU.mult, ALU.subtract
+            )
+
+        xm_bf = [keep.tile([P, b - a, PACK], BF16, name="xm_bf%d" % a, align_bytes=64) for a, b in XM_CHUNKS]
+        xm_codes = [keep.tile([P, b - a], U32, name="xm_codes%d" % a, align_bytes=64) for a, b in XM_CHUNKS]
+        xm_scales = [keep.tile([P, b - a], U8, name="xm_scales%d" % a, align_bytes=64) for a, b in XM_CHUNKS]
+
+        def weave_xm(c):
+            nc.scalar.copy(
+                xm_bf[c][:].rearrange("p (c i) j -> p c j i", i=4), xm_raw[c][:].rearrange("p j (c i) -> p c j i", i=4)
+            )
+
+        def quantize_xm(c):
+            nc.vector.quantize_mx(
+                out=xm_codes[c][:].bitcast(E4M3), scales=xm_scales[c][:], in_=xm_bf[c][:].rearrange("p d j -> p (d j)")
+            )
+
+        weave_xm(0)
+        weave_xm(1)
+        nc.vector.tensor_copy(
+            g_bf[:].rearrange("p (c i) j -> p c j i", i=4), g_planes[:].rearrange("p j (c i) -> p c j i", i=4)
+        )
+        quantize_xm(0)
+        nc.vector.quantize_mx(out=g_codes[:].bitcast(E5M2), scales=g_scales[:], in_=g_bf[:].rearrange("p i j -> p (i j)"))
+        quantize_xm(1)
+
+        def product(m):
+            c = max(k for k, (a, b) in enumerate(XM_CHUNKS) if a <= m * P)
+            cols = slice(m * P - XM_CHUNKS[c][0], (m + 1) * P - XM_CHUNKS[c][0])
+            acc = psum_o.tile([P, N], F32, name="acc")
+            nc.tensor.matmul_mx(
+                out=acc[:],
+                lhsT=xm_codes[c][:, cols].bitcast(E4M3),
+                lhsT_scale=xm_scales[c][:, cols],
+                rhs=g_codes[:].bitcast(E5M2),
+                rhs_scale=g_scales[:],
+                start=True,
+                stop=True,
+            )
+            dw = ring.tile([P, N], F32, name="dw")
+            nc.scalar.copy(dw[:], acc[:])
+            window = windows[m % WINDOWS]
+            nc.vector.tensor_copy(window[:].indirect(offsets[:]), dw[:])
+            nc.sync.dma_start(out=out[m * P : (m + 1) * P, :], in_=window[:])
+
+        product(0)
+        product(1)
+        weave_xm(2)
+        quantize_xm(2)
+        for m in range(2, D_TILES):
+            product(m)

@@ -22,7 +22,10 @@ PASSES = D // K_PASS
 HALF = R // 2
 D_TILES = D // P
 WINDOWS = 4
-XM_CHUNKS = ((0, 256), (256, 512), (512, 1024))
+NH = N // 2
+X_SCALAR = (64, 44)
+XM_LOADS = ((0, 256), (256, 512), (512, 1024))
+XM_CHUNKS = ((0, 128), (128, 256), (256, 512), (512, 1024))
 
 
 def tile_attend_glse_w_kernel(tc, xT, wT, y, lse, wt, xm, offs, out):
@@ -30,16 +33,16 @@ def tile_attend_glse_w_kernel(tc, xT, wT, y, lse, wt, xm, offs, out):
     with ExitStack() as ctx:
         keep = ctx.enter_context(tc.tile_pool(name="keep", bufs=1))
         ring = ctx.enter_context(tc.tile_pool(name="ring", bufs=3))
-        psum_a = ctx.enter_context(tc.psum_pool(name="psum_a", bufs=1))
-        psum_o = ctx.enter_context(tc.psum_pool(name="psum_o", bufs=4))
+        psum = ctx.enter_context(tc.psum_pool(name="psum", bufs=1))
 
         offsets = keep.tile([P, N // 16], U16, name="offsets")
         w_raw = [keep.tile([P, T], F32, name="w_raw%d" % u) for u in range(PASSES * PACK)]
-        x_raw = [keep.tile([P, PACK, HALF], F32, name="x_raw%d" % u) for u in range(PASSES * 2)]
-        y_raw = [keep.tile([P, 2, N], F32, name="y_raw%d" % u) for u in range(2)]
-        xm_raw = [keep.tile([P, PACK, b - a], F32, name="xm_raw%d" % a) for a, b in XM_CHUNKS]
+        x_pieces = ((0, 0, R), (1, 0, R))
+        x_raw = [keep.tile([P, PACK, b - a], F32, name="x_raw%d" % u) for u, (g, a, b) in enumerate(x_pieces)]
+        y_raw = [keep.tile([P, N], F32, name="y_raw%d" % j) for j in range(PACK)]
+        xm_raw = [keep.tile([P, PACK, b - a], F32, name="xm_raw%d" % a) for a, b in XM_LOADS]
         lse_sb = keep.tile([P, PACK], F32, name="lse_sb")
-        neg_lse = keep.tile([P, PACK], F32, name="neg_lse")
+        neg_lse = keep.tile([P, PACK], F32, name="neg_lse", align_bytes=64)
         wt_sb = keep.tile([P, PACK], F32, name="wt_sb")
         windows = [keep.tile([P, T], F32, name="window%d" % u) for u in range(WINDOWS)]
 
@@ -52,23 +55,26 @@ def tile_attend_glse_w_kernel(tc, xT, wT, y, lse, wt, xm, offs, out):
             nc.sync.dma_start(out=w_raw[u][:], in_=w_planes[u // PACK, u % PACK])
 
         def load_x(u):
-            g, h = divmod(u, 2)
-            nc.sync.dma_start(out=x_raw[u][:], in_=x_rows[g][:, :, h * HALF : (h + 1) * HALF])
+            g, a, b = x_pieces[u]
+            nc.sync.dma_start(out=x_raw[u][:], in_=x_rows[g][:, :, a:b])
 
         load_w(0)
         nc.sync.dma_start(offsets[:], offs)
-        nc.sync.dma_start(out=lse_sb[:], in_=lse[0].rearrange("(p j) o -> p (j o)", j=PACK))
-        nc.sync.dma_start(out=wt_sb[:], in_=wt[0].rearrange("(p j) o -> p (j o)", j=PACK))
-        load_x(0)
+        nc.scalar.dma_start(out=lse_sb[:], in_=lse[0].rearrange("(p j) o -> p (j o)", j=PACK))
+        nc.scalar.dma_start(out=wt_sb[:], in_=wt[0].rearrange("(p j) o -> p (j o)", j=PACK))
         for u in range(1, PASSES * PACK):
             load_w(u)
-        for u in range(1, PASSES * 2):
-            load_x(u)
-        for u in range(2):
-            nc.sync.dma_start(out=y_raw[u][:], in_=y_rows[:, 2 * u : 2 * u + 2, :])
-        for c, (a, b) in enumerate(XM_CHUNKS):
+        load_x(0)
+        load_x(1)
+        for j in range(PACK):
+            nc.sync.dma_start(out=y_raw[j][:], in_=y_rows[:, j, :])
+        for c, (a, b) in enumerate(XM_LOADS):
             nc.sync.dma_start(out=xm_raw[c][:], in_=xm_rows[:, :, a:b])
 
+        g_codes = keep.tile([P, N], U32, name="g_codes", align_bytes=64)
+        g_scales = keep.tile([P, N], U8, name="g_scales", align_bytes=64)
+        nc.vector.memset(g_codes[:, NH:], 0)
+        nc.vector.memset(g_scales[:, NH:], 0)
         for window in windows:
             nc.vector.memset(window[:], 0.0)
         nc.scalar.activation(neg_lse[:], lse_sb[:], ACT.Copy, scale=-1.0)
@@ -88,12 +94,11 @@ def tile_attend_glse_w_kernel(tc, xT, wT, y, lse, wt, xm, offs, out):
                 out=w_codes[g][:].bitcast(E4M3), scales=w_scales[g][:], in_=w_bf[g][:].rearrange("p n t -> p (n t)")
             )
 
-        def weave_x(u, copy):
-            g, h = divmod(u, 2)
-            s_cols = slice(h * P // 2, (h + 1) * P // 2)
+        def weave_x(u, s0, s1, copy):
+            g, a, b = x_pieces[u]
             copy(
-                x_bf[g][:, :, s_cols, :].rearrange("p j s t -> p s t j"),
-                x_raw[u][:].rearrange("p t (s j) -> p s t j", j=PACK),
+                x_bf[g][:, :, s0:s1, :].rearrange("p j s t -> p s t j"),
+                x_raw[u][:, :, PACK * s0 - a : PACK * s1 - a].rearrange("p t (s j) -> p s t j", j=PACK),
             )
 
         def quantize_x(g, j0, j1):
@@ -104,78 +109,90 @@ def tile_attend_glse_w_kernel(tc, xT, wT, y, lse, wt, xm, offs, out):
                 in_=x_bf[g][:, j0:j1].rearrange("p j s t -> p (j s t)"),
             )
 
-        scores = [psum_a.tile([P, N], F32, name="score%d" % j) for j in range(PACK)]
+        scores = [[psum.tile([P, NH], F32, name="bank%d" % (PACK * h + j)) for j in range(PACK)] for h in range(2)]
 
-        def score_pass(g, j):
+        def score_pass(g, h, j, start):
             cols = slice(j * P, (j + 1) * P)
+            slots = slice(h * NH, (h + 1) * NH)
             nc.tensor.matmul_mx(
-                out=scores[j][:],
+                out=scores[h][j][:],
                 lhsT=x_codes[g][:, cols].bitcast(E4M3),
                 lhsT_scale=x_scales[g][:, cols],
-                rhs=w_codes[g][:].bitcast(E4M3),
-                rhs_scale=w_scales[g][:],
-                start=(g == 0),
-                stop=(g == PASSES - 1),
+                rhs=w_codes[g][:, slots].bitcast(E4M3),
+                rhs_scale=w_scales[g][:, slots],
+                start=start,
+                stop=not start,
             )
 
-        weave_x(0, nc.scalar.copy)
-        for u in range(PACK):
-            gather_w(u)
-        quantize_w(0)
-        for u in range(PACK, 2 * PACK):
-            gather_w(u)
-        weave_x(1, nc.scalar.copy)
-        weave_x(2, nc.scalar.copy)
-        quantize_w(1)
-        quantize_x(0, 0, PACK)
+        for g in range(PASSES):
+            for t in range(PACK):
+                gather_w(g * PACK + t)
+            quantize_w(g)
+        weave_x(0, 0, X_SCALAR[0], nc.scalar.copy)
+        weave_x(0, X_SCALAR[0], P, nc.vector.tensor_copy)
+        for j in range(0, PACK, 2):
+            quantize_x(0, j, j + 2)
         for j in range(PACK):
-            score_pass(0, j)
-        weave_x(3, nc.vector.tensor_copy)
+            score_pass(0, 0, j, True)
+        weave_x(1, 0, X_SCALAR[1], nc.scalar.copy)
+        weave_x(1, X_SCALAR[1], P, nc.vector.tensor_copy)
+        for j0, j1 in ((0, 1), (1, 2), (2, PACK)):
+            quantize_x(1, j0, j1)
+            for j in range(j0, j1):
+                score_pass(1, 0, j, False)
         for j in range(PACK):
-            quantize_x(1, j, j + 1)
-            score_pass(1, j)
+            first = 0 if j < 2 else 1
+            score_pass(first, 1, j, True)
+            score_pass(1 - first, 1, j, False)
 
         yw = keep.tile([P, PACK, N], F32, name="yw")
-        prob = keep.tile([P, PACK, N], F32, name="prob")
-        g_planes = keep.tile([P, PACK, N], BF16, name="g_planes")
-        g_bf = keep.tile([P, N, PACK], BF16, name="g_bf", align_bytes=64)
-        g_codes = keep.tile([P, N], U32, name="g_codes", align_bytes=64)
-        g_scales = keep.tile([P, N], U8, name="g_scales", align_bytes=64)
-        for j in range(PACK):
-            nc.scalar.activation(prob[:, j, :], scores[j][:], ACT.Exp, bias=neg_lse[:, j : j + 1])
-            nc.vector.tensor_scalar(yw[:, j, :], y_raw[j // 2][:, j % 2, :], wt_sb[:, j : j + 1], None, ALU.mult)
-        for j in range(PACK):
-            nc.vector.scalar_tensor_tensor(
-                g_planes[:, j, :], prob[:, j, :], wt_sb[:, j : j + 1], yw[:, j, :], ALU.mult, ALU.subtract
-            )
-
-        xm_bf = [keep.tile([P, b - a, PACK], BF16, name="xm_bf%d" % a, align_bytes=64) for a, b in XM_CHUNKS]
+        prob = [keep.tile([P, PACK, NH], F32, name="prob%d" % h, align_bytes=64) for h in range(2)]
+        g_planes = [keep.tile([P, PACK, NH], BF16, name="g_planes%d" % h) for h in range(2)]
+        g_bf = [keep.tile([P, NH, PACK], BF16, name="g_bf%d" % h, align_bytes=64) for h in range(2)]
+        xm_bf = {}
         xm_codes = [keep.tile([P, b - a], U32, name="xm_codes%d" % a, align_bytes=64) for a, b in XM_CHUNKS]
         xm_scales = [keep.tile([P, b - a], U8, name="xm_scales%d" % a, align_bytes=64) for a, b in XM_CHUNKS]
 
-        def weave_xm(c):
-            nc.scalar.copy(
-                xm_bf[c][:].rearrange("p (c i) j -> p c j i", i=4), xm_raw[c][:].rearrange("p j (c i) -> p c j i", i=4)
-            )
+        def exp_half(h):
+            for j in range(PACK):
+                nc.scalar.activation(prob[h][:, j, :], scores[h][j][:], ACT.Exp, bias=neg_lse[:, j : j + 1])
+
+        def gradient_half(h):
+            for j in range(PACK):
+                nc.vector.scalar_tensor_tensor(
+                    g_planes[h][:, j, :],
+                    prob[h][:, j, :],
+                    wt_sb[:, j : j + 1],
+                    yw[:, j, h * NH : (h + 1) * NH],
+                    ALU.mult,
+                    ALU.subtract,
+                )
+
+        def weave_xm(c, tag):
+            a, b = XM_CHUNKS[c]
+            xm_bf[c] = keep.tile([P, b - a, PACK], BF16, name="xm_bf%d" % c, tag=tag, align_bytes=64)
+            u = max(k for k, (a0, b0) in enumerate(XM_LOADS) if a0 <= a)
+            raw = xm_raw[u][:, :, a - XM_LOADS[u][0] : b - XM_LOADS[u][0]]
+            nc.scalar.copy(xm_bf[c][:].rearrange("p (c i) j -> p c j i", i=4), raw.rearrange("p j (c i) -> p c j i", i=4))
 
         def quantize_xm(c):
             nc.vector.quantize_mx(
                 out=xm_codes[c][:].bitcast(E4M3), scales=xm_scales[c][:], in_=xm_bf[c][:].rearrange("p d j -> p (d j)")
             )
 
-        weave_xm(0)
-        weave_xm(1)
-        nc.vector.tensor_copy(
-            g_bf[:].rearrange("p (c i) j -> p c j i", i=4), g_planes[:].rearrange("p j (c i) -> p c j i", i=4)
-        )
-        quantize_xm(0)
-        nc.vector.quantize_mx(out=g_codes[:].bitcast(E5M2), scales=g_scales[:], in_=g_bf[:].rearrange("p i j -> p (i j)"))
-        quantize_xm(1)
+        def weave_g(h, copy):
+            copy(g_bf[h][:].rearrange("p (c i) j -> p c j i", i=4), g_planes[h][:].rearrange("p j (c i) -> p c j i", i=4))
 
-        def product(m):
+        def quantize_g(h):
+            cols = slice(h * NH, (h + 1) * NH)
+            nc.vector.quantize_mx(
+                out=g_codes[:, cols].bitcast(E5M2), scales=g_scales[:, cols], in_=g_bf[h][:].rearrange("p i j -> p (i j)")
+            )
+
+        def product(m, bank):
             c = max(k for k, (a, b) in enumerate(XM_CHUNKS) if a <= m * P)
             cols = slice(m * P - XM_CHUNKS[c][0], (m + 1) * P - XM_CHUNKS[c][0])
-            acc = psum_o.tile([P, N], F32, name="acc")
+            acc = psum.tile([P, N], F32, name="acc", tag="bank%d" % bank)
             nc.tensor.matmul_mx(
                 out=acc[:],
                 lhsT=xm_codes[c][:, cols].bitcast(E4M3),
@@ -185,15 +202,42 @@ def tile_attend_glse_w_kernel(tc, xT, wT, y, lse, wt, xm, offs, out):
                 start=True,
                 stop=True,
             )
-            dw = ring.tile([P, N], F32, name="dw")
-            nc.scalar.copy(dw[:], acc[:])
-            window = windows[m % WINDOWS]
-            nc.vector.tensor_copy(window[:].indirect(offsets[:]), dw[:])
-            nc.sync.dma_start(out=out[m * P : (m + 1) * P, :], in_=window[:])
+            return acc
 
-        product(0)
-        product(1)
-        weave_xm(2)
+        def scatter(m, acc, lo, hi, dw):
+            nc.scalar.copy(dw[:], acc[:, lo:hi])
+            nc.vector.tensor_copy(windows[m % WINDOWS][:].indirect(offsets[:, lo // 16 : hi // 16]), dw[:])
+
+        def store(m):
+            nc.sync.dma_start(out=out[m * P : (m + 1) * P, :], in_=windows[m % WINDOWS][:])
+
+        for j in range(2):
+            nc.scalar.activation(yw[:, j, :], y_raw[j][:], ACT.Copy, scale=wt_sb[:, j : j + 1])
+        for j in range(2, PACK):
+            nc.vector.tensor_scalar(yw[:, j, :], y_raw[j][:], wt_sb[:, j : j + 1], None, ALU.mult)
+        exp_half(0)
+        weave_xm(0, "xm_bf0")
+        exp_half(1)
+        gradient_half(0)
+        weave_g(0, nc.vector.tensor_copy)
+        quantize_xm(0)
+        quantize_g(0)
+        early0 = product(0, 0)
+        gradient_half(1)
+        weave_xm(1, "neg_lse")
+        quantize_xm(1)
+        early1 = product(1, 1)
+        scatter(0, early0, 0, NH, keep.tile([P, NH], F32, name="dw_a0"))
+        weave_g(1, nc.scalar.copy)
+        quantize_g(1)
+        scatter(1, early1, 0, NH, keep.tile([P, NH], F32, name="dw_a1", tag="g_planes1"))
+        weave_xm(2, "prob1")
         quantize_xm(2)
+        for m in range(2):
+            scatter(m, product(m, 2 + m), NH, N, keep.tile([P, NH], F32, name="dw_b%d" % m))
+            store(m)
+        weave_xm(3, "xm_codes0")
+        quantize_xm(3)
         for m in range(2, D_TILES):
-            product(m)
+            scatter(m, product(m, (2 + m) % 8), 0, N, ring.tile([P, N], F32, name="dw"))
+            store(m)

@@ -23,9 +23,9 @@ HALF = R // 2
 D_TILES = D // P
 WINDOWS = 4
 NH = N // 2
-X_SCALAR = (64, 44)
-XM_LOADS = ((0, 256), (256, 512), (512, 1024))
-XM_CHUNKS = ((0, 128), (128, 256), (256, 512), (512, 1024))
+X_SCALAR = (68, 44)
+XM_LOADS = ((0, 384), (384, 1024))
+XM_CHUNKS = ((0, 128), (128, 256), (256, 384), (384, 512), (512, 1024))
 
 
 def tile_attend_glse_w_kernel(tc, xT, wT, y, lse, wt, xm, offs, out):
@@ -80,6 +80,7 @@ def tile_attend_glse_w_kernel(tc, xT, wT, y, lse, wt, xm, offs, out):
         nc.scalar.activation(neg_lse[:], lse_sb[:], ACT.Copy, scale=-1.0)
 
         w_bf = [keep.tile([P, N, PACK], BF16, name="w_bf%d" % g, align_bytes=64) for g in range(PASSES)]
+        w_cols = [keep.tile([P, PACK - 2 * g, N], BF16, name="w_cols%d" % g) for g in range(PASSES)]
         w_codes = [keep.tile([P, N], U32, name="w_codes%d" % g, align_bytes=64) for g in range(PASSES)]
         w_scales = [keep.tile([P, N], U8, name="w_scales%d" % g, align_bytes=64) for g in range(PASSES)]
         x_bf = [keep.tile([P, PACK, P, PACK], BF16, name="x_bf%d" % g, align_bytes=64) for g in range(PASSES)]
@@ -87,7 +88,13 @@ def tile_attend_glse_w_kernel(tc, xT, wT, y, lse, wt, xm, offs, out):
         x_scales = [keep.tile([P, R], U8, name="x_scales%d" % g, align_bytes=64) for g in range(PASSES)]
 
         def gather_w(u):
-            nc.vector.tensor_copy(w_bf[u // PACK][:, :, u % PACK], w_raw[u][:].indirect(offsets[:]))
+            nc.vector.tensor_copy(w_cols[u // PACK][:, u % PACK, :], w_raw[u][:].indirect(offsets[:]))
+
+        def weave_w(g, t0, t1, copy):
+            copy(
+                w_bf[g][:, :, t0:t1].rearrange("p (c i) t -> p c t i", i=4),
+                w_cols[g][:, t0:t1, :].rearrange("p t (c i) -> p c t i", i=4),
+            )
 
         def quantize_w(g):
             nc.vector.quantize_mx(
@@ -124,10 +131,16 @@ def tile_attend_glse_w_kernel(tc, xT, wT, y, lse, wt, xm, offs, out):
                 stop=not start,
             )
 
-        for g in range(PASSES):
-            for t in range(PACK):
-                gather_w(g * PACK + t)
-            quantize_w(g)
+        for u in range(PACK):
+            gather_w(u)
+        weave_w(0, 0, PACK, nc.scalar.copy)
+        gather_w(PACK)
+        gather_w(PACK + 1)
+        weave_w(1, 0, 2, nc.scalar.copy)
+        quantize_w(0)
+        for t in range(2, PACK):
+            nc.vector.tensor_copy(w_bf[1][:, :, t], w_raw[PACK + t][:].indirect(offsets[:]))
+        quantize_w(1)
         weave_x(0, 0, X_SCALAR[0], nc.scalar.copy)
         weave_x(0, X_SCALAR[0], P, nc.vector.tensor_copy)
         for j in range(0, PACK, 2):
@@ -237,7 +250,9 @@ def tile_attend_glse_w_kernel(tc, xT, wT, y, lse, wt, xm, offs, out):
             scatter(m, product(m, 2 + m), NH, N, keep.tile([P, NH], F32, name="dw_b%d" % m))
             store(m)
         weave_xm(3, "xm_codes0")
+        weave_xm(4, "xm_scales0")
         quantize_xm(3)
+        quantize_xm(4)
         for m in range(2, D_TILES):
             scatter(m, product(m, (2 + m) % 8), 0, N, ring.tile([P, N], F32, name="dw"))
             store(m)

from contextlib import ExitStack

import concourse.mybir as mybir

N, T, D, R = 512, 2048, 1024, 512
FLOPS = 2 * 2 * N * D * R

F32 = mybir.dt.float32
BF16 = mybir.dt.bfloat16
U32 = mybir.dt.uint32
U16 = mybir.dt.uint16
U8 = mybir.dt.uint8
E4M3 = mybir.dt.float8_e4m3fn_x4
E5M2 = mybir.dt.float8_e5m2_x4
ACT = mybir.ActivationFunctionType
ALU = mybir.AluOpType

P = 128
PACK = 4
K_PASS = P * PACK
PASSES = D // K_PASS
HALF = R // 2
D_TILES = D // P
WINDOWS = 4
NH = N // 2
X_SCALAR = (68, 44)
XM_LOADS = ((0, 384), (384, 1024))
XM_CHUNKS = ((0, 128), (128, 256), (256, 384), (384, 512), (512, 1024))


def tile_attend_glse_w_kernel(tc, xT, wT, y, lse, wt, xm, offs, out):
    nc = tc.nc
    with ExitStack() as ctx:
        keep = ctx.enter_context(tc.tile_pool(name="keep", bufs=1))
        ring = ctx.enter_context(tc.tile_pool(name="ring", bufs=3))
        psum = ctx.enter_context(tc.psum_pool(name="psum", bufs=1))

        offsets = keep.tile([P, N // 16], U16, name="offsets")
        w_raw = [keep.tile([P, T], F32, name="w_raw%d" % u) for u in range(PASSES * PACK)]
        x_pieces = ((0, 0, R), (1, 0, R))
        x_raw = [keep.tile([P, PACK, b - a], F32, name="x_raw%d" % u) for u, (g, a, b) in enumerate(x_pieces)]
        y_raw = [keep.tile([P, N], F32, name="y_raw%d" % j) for j in range(PACK)]
        xm_raw = [keep.tile([P, PACK, b - a], F32, name="xm_raw%d" % a) for a, b in XM_LOADS]
        lse_sb = keep.tile([P, PACK], F32, name="lse_sb")
        neg_lse = keep.tile([P, PACK], F32, name="neg_lse", align_bytes=64)
        wt_sb = keep.tile([P, PACK], F32, name="wt_sb")
        windows = [keep.tile([P, T], F32, name="window%d" % u) for u in range(WINDOWS)]

        w_planes = wT.rearrange("(g p t) c -> g t p c", p=P, t=PACK)
        x_rows = xT[0].rearrange("(g p t) r -> g p t r", p=P, t=PACK)
        y_rows = y[0].rearrange("(p j) i -> p j i", j=PACK)
        xm_rows = xm[0].rearrange("(p j) d -> p j d", j=PACK)

        def load_w(u):
            nc.sync.dma_start(out=w_raw[u][:], in_=w_planes[u // PACK, u % PACK])

        def load_x(u):
            g, a, b = x_pieces[u]
            nc.sync.dma_start(out=x_raw[u][:], in_=x_rows[g][:, :, a:b])

        load_w(0)
        nc.sync.dma_start(offsets[:], offs)
        nc.scalar.dma_start(out=lse_sb[:], in_=lse[0].rearrange("(p j) o -> p (j o)", j=PACK))
        nc.scalar.dma_start(out=wt_sb[:], in_=wt[0].rearrange("(p j) o -> p (j o)", j=PACK))
        for u in range(1, PASSES * PACK):
            load_w(u)
        load_x(0)
        load_x(1)
        for j in range(PACK):
            nc.sync.dma_start(out=y_raw[j][:], in_=y_rows[:, j, :])
        for c, (a, b) in enumerate(XM_LOADS):
            nc.sync.dma_start(out=xm_raw[c][:], in_=xm_rows[:, :, a:b])

        g_codes = keep.tile([P, N], U32, name="g_codes", align_bytes=64)
        g_scales = keep.tile([P, N], U8, name="g_scales", align_bytes=64)
        nc.vector.memset(g_codes[:, NH:], 0)
        nc.vector.memset(g_scales[:, NH:], 0)
        for window in windows:
            nc.vector.memset(window[:], 0.0)
        nc.scalar.activation(neg_lse[:], lse_sb[:], ACT.Copy, scale=-1.0)

        w_bf = [keep.tile([P, N, PACK], BF16, name="w_bf%d" % g, align_bytes=64) for g in range(PASSES)]
        w_cols = [keep.tile([P, PACK - 2 * g, N], BF16, name="w_cols%d" % g) for g in range(PASSES)]
        w_codes = [keep.tile([P, N], U32, name="w_codes%d" % g, align_bytes=64) for g in range(PASSES)]
        w_scales = [keep.tile([P, N], U8, name="w_scales%d" % g, align_bytes=64) for g in range(PASSES)]
        x_bf = [keep.tile([P, PACK, P, PACK], BF16, name="x_bf%d" % g, align_bytes=64) for g in range(PASSES)]
        x_codes = [keep.tile([P, R], U32, name="x_codes%d" % g, align_bytes=64) for g in range(PASSES)]
        x_scales = [keep.tile([P, R], U8, name="x_scales%d" % g, align_bytes=64) for g in range(PASSES)]

        def gather_w(u):
            nc.vector.tensor_copy(w_cols[u // PACK][:, u % PACK, :], w_raw[u][:].indirect(offsets[:]))

        def weave_w(g, t0, t1, copy):
            copy(
                w_bf[g][:, :, t0:t1].rearrange("p (c i) t -> p c t i", i=4),
                w_cols[g][:, t0:t1, :].rearrange("p t (c i) -> p c t i", i=4),
            )

        def quantize_w(g):
            nc.vector.quantize_mx(
                out=w_codes[g][:].bitcast(E4M3), scales=w_scales[g][:], in_=w_bf[g][:].rearrange("p n t -> p (n t)")
            )

        def weave_x(u, s0, s1, copy):
            g, a, b = x_pieces[u]
            copy(
                x_bf[g][:, :, s0:s1, :].rearrange("p j s t -> p s t j"),
                x_raw[u][:, :, PACK * s0 - a : PACK * s1 - a].rearrange("p t (s j) -> p s t j", j=PACK),
            )

        def quantize_x(g, j0, j1):
            cols = slice(j0 * P, j1 * P)
            nc.vector.quantize_mx(
                out=x_codes[g][:, cols].bitcast(E4M3),
                scales=x_scales[g][:, cols],
                in_=x_bf[g][:, j0:j1].rearrange("p j s t -> p (j s t)"),
            )

        scores = [[psum.tile([P, NH], F32, name="bank%d" % (PACK * h + j)) for j in range(PACK)] for h in range(2)]

        def score_pass(g, h, j, start):
            cols = slice(j * P, (j + 1) * P)
            slots = slice(h * NH, (h + 1) * NH)
            nc.tensor.matmul_mx(
                out=scores[h][j][:],
                lhsT=x_codes[g][:, cols].bitcast(E4M3),
                lhsT_scale=x_scales[g][:, cols],
                rhs=w_codes[g][:, slots].bitcast(E4M3),
                rhs_scale=w_scales[g][:, slots],
                start=start,
                stop=not start,
            )

        for u in range(PACK):
            gather_w(u)
        weave_w(0, 0, PACK, nc.scalar.copy)
        gather_w(PACK)
        gather_w(PACK + 1)
        weave_w(1, 0, 2, nc.scalar.copy)
        quantize_w(0)
        for t in range(2, PACK):
            nc.vector.tensor_copy(w_bf[1][:, :, t], w_raw[PACK + t][:].indirect(offsets[:]))
        quantize_w(1)
        weave_x(0, 0, X_SCALAR[0], nc.scalar.copy)
        weave_x(0, X_SCALAR[0], P, nc.vector.tensor_copy)
        for j in range(0, PACK, 2):
            quantize_x(0, j, j + 2)
        for j in range(PACK):
            score_pass(0, 0, j, True)
        weave_x(1, 0, X_SCALAR[1], nc.scalar.copy)
        weave_x(1, X_SCALAR[1], P, nc.vector.tensor_copy)
        for j0, j1 in ((0, 1), (1, 2), (2, PACK)):
            quantize_x(1, j0, j1)
            for j in range(j0, j1):
                score_pass(1, 0, j, False)
        for j in range(PACK):
            first = 0 if j < 2 else 1
            score_pass(first, 1, j, True)
            score_pass(1 - first, 1, j, False)

        yw = keep.tile([P, PACK, N], F32, name="yw")
        prob = [keep.tile([P, PACK, NH], F32, name="prob%d" % h, align_bytes=64) for h in range(2)]
        g_planes = [keep.tile([P, PACK, NH], BF16, name="g_planes%d" % h) for h in range(2)]
        g_bf = [keep.tile([P, NH, PACK], BF16, name="g_bf%d" % h, align_bytes=64) for h in range(2)]
        xm_bf = {}
        xm_codes = [keep.tile([P, b - a], U32, name="xm_codes%d" % a, align_bytes=64) for a, b in XM_CHUNKS]
        xm_scales = [keep.tile([P, b - a], U8, name="xm_scales%d" % a, align_bytes=64) for a, b in XM_CHUNKS]

        def exp_half(h):
            for j in range(PACK):
                nc.scalar.activation(prob[h][:, j, :], scores[h][j][:], ACT.Exp, bias=neg_lse[:, j : j + 1])

        def gradient_half(h):
            for j in range(PACK):
                nc.vector.scalar_tensor_tensor(
                    g_planes[h][:, j, :],
                    prob[h][:, j, :],
                    wt_sb[:, j : j + 1],
                    yw[:, j, h * NH : (h + 1) * NH],
                    ALU.mult,
                    ALU.subtract,
                )

        def weave_xm(c, tag):
            a, b = XM_CHUNKS[c]
            xm_bf[c] = keep.tile([P, b - a, PACK], BF16, name="xm_bf%d" % c, tag=tag, align_bytes=64)
            u = max(k for k, (a0, b0) in enumerate(XM_LOADS) if a0 <= a)
            raw = xm_raw[u][:, :, a - XM_LOADS[u][0] : b - XM_LOADS[u][0]]
            nc.scalar.copy(xm_bf[c][:].rearrange("p (c i) j -> p c j i", i=4), raw.rearrange("p j (c i) -> p c j i", i=4))

        def quantize_xm(c):
            nc.vector.quantize_mx(
                out=xm_codes[c][:].bitcast(E4M3), scales=xm_scales[c][:], in_=xm_bf[c][:].rearrange("p d j -> p (d j)")
            )

        def weave_g(h, copy):
            copy(g_bf[h][:].rearrange("p (c i) j -> p c j i", i=4), g_planes[h][:].rearrange("p j (c i) -> p c j i", i=4))

        def quantize_g(h):
            cols = slice(h * NH, (h + 1) * NH)
            nc.vector.quantize_mx(
                out=g_codes[:, cols].bitcast(E5M2), scales=g_scales[:, cols], in_=g_bf[h][:].rearrange("p i j -> p (i j)")
            )

        def product(m, bank):
            c = max(k for k, (a, b) in enumerate(XM_CHUNKS) if a <= m * P)
            cols = slice(m * P - XM_CHUNKS[c][0], (m + 1) * P - XM_CHUNKS[c][0])
            acc = psum.tile([P, N], F32, name="acc", tag="bank%d" % bank)
            nc.tensor.matmul_mx(
                out=acc[:],
                lhsT=xm_codes[c][:, cols].bitcast(E4M3),
                lhsT_scale=xm_scales[c][:, cols],
                rhs=g_codes[:].bitcast(E5M2),
                rhs_scale=g_scales[:],
                start=True,
                stop=True,
            )
            return acc

        def scatter(m, acc, lo, hi, dw):
            nc.scalar.copy(dw[:], acc[:, lo:hi])
            nc.vector.tensor_copy(windows[m % WINDOWS][:].indirect(offsets[:, lo // 16 : hi // 16]), dw[:])

        def store(m):
            nc.sync.dma_start(out=out[m * P : (m + 1) * P, :], in_=windows[m % WINDOWS][:])

        for j in range(2):
            nc.scalar.activation(yw[:, j, :], y_raw[j][:], ACT.Copy, scale=wt_sb[:, j : j + 1])
        for j in range(2, PACK):
            nc.vector.tensor_scalar(yw[:, j, :], y_raw[j][:], wt_sb[:, j : j + 1], None, ALU.mult)
        exp_half(0)
        weave_xm(0, "xm_bf0")
        exp_half(1)
        gradient_half(0)
        weave_g(0, nc.vector.tensor_copy)
        quantize_xm(0)
        quantize_g(0)
        early0 = product(0, 0)
        gradient_half(1)
        weave_xm(1, "neg_lse")
        quantize_xm(1)
        early1 = product(1, 1)
        scatter(0, early0, 0, NH, keep.tile([P, NH], F32, name="dw_a0"))
        weave_g(1, nc.scalar.copy)
        quantize_g(1)
        scatter(1, early1, 0, NH, keep.tile([P, NH], F32, name="dw_a1", tag="g_planes1"))
        weave_xm(2, "prob1")
        quantize_xm(2)
        for m in range(2):
            scatter(m, product(m, 2 + m), NH, N, keep.tile([P, NH], F32, name="dw_b%d" % m))
            store(m)
        weave_xm(3, "xm_codes0")
        weave_xm(4, "xm_scales0")
        quantize_xm(3)
        quantize_xm(4)
        for m in range(2, D_TILES):
            scatter(m, product(m, (2 + m) % 8), 0, N, ring.tile([P, N], F32, name="dw"))
            store(m)
